import numpy as np
import ml_dtypes


def mxq(x, axis, fmt="e4m3"):
    dtype, down = {"e4m3": (ml_dtypes.float8_e4m3fn, 7), "e5m2": (ml_dtypes.float8_e5m2, 14)}[fmt]
    v = np.moveaxis(np.asarray(x, np.float32).astype(ml_dtypes.bfloat16).astype(np.float64), axis, -1)
    blocks = v.reshape(v.shape[:-1] + (-1, 32))
    amax = np.abs(blocks).max(-1, keepdims=True)
    byte = np.maximum(np.where(amax > 0, np.frexp(amax)[1] - 1 + 127, 0) - down, 1)
    scale = np.exp2(byte - 127.0)
    codes = (blocks / scale).astype(np.float32).astype(dtype).astype(np.float64)
    return np.moveaxis((codes * scale).reshape(v.shape), -1, axis)


WIDE = False


def mx_kscale(k):
    if not WIDE:
        return np.ones(k)
    levels = np.array([10, -10, 5, -5, 0])
    if k % 512:
        return np.exp2(np.random.permutation(np.resize(levels, k // 32))).repeat(32)
    a = np.empty((k // 512, 16))
    for p in range(k // 512):
        a[p, :8] = np.random.permutation(np.resize(levels, 8))
        for g in range(8):
            far = levels[np.abs(levels - a[p, g]) >= 10]
            a[p, g + 8] = far[np.random.randint(len(far))]
    return np.exp2(a.ravel()).repeat(32)


def f64(x):
    return np.asarray(x).astype(np.float64)


def striped8(idx):
    return np.asarray(idx).reshape(8, -1, 16).transpose(0, 2, 1).reshape(128, -1).astype(np.uint16)


def unstriped8(offs):
    return offs.reshape(8, 16, -1).transpose(0, 2, 1).reshape(8, -1).astype(np.int64)


def pick8(x, idx, run):
    r = np.arange(len(x))
    return x[r[:, None], idx[r % (8 * run) // run]]


E2M1 = np.array([0.0, 0.5, 1.0, 1.5, 2.0, 3.0, 4.0, 6.0, -0.0, -0.5, -1.0, -1.5, -2.0, -3.0, -4.0, -6.0])


def pack_weight(w, fmt):
    k, n = w.shape
    w = f64(np.asarray(w, np.float32).astype(ml_dtypes.bfloat16)).reshape(k // 32, 32, n)
    amax = np.abs(w).max(1)
    if fmt == "e4m3":
        byte = np.frexp(amax)[1] - 1 + 127 - 7
    else:
        mant, ex = np.frexp(amax / 6.0)
        byte = np.where(mant > 0.5, ex, ex - 1) + 127
    byte = np.clip(np.where(amax > 0, byte, 1), 1, 254)
    scaled = (w * np.exp2(127.0 - byte)[:, None, :]).reshape(k, n).astype(np.float32)
    by_word = np.ascontiguousarray(scaled.reshape(k // 512, 128, 4, n).transpose(0, 1, 3, 2))
    if fmt == "e4m3":
        words = by_word.astype(ml_dtypes.float8_e4m3fn).view(np.uint8)
    else:
        c = by_word.astype(ml_dtypes.float4_e2m1fn).view(np.uint8) & 0xF
        words = (c[..., 0::2] | (c[..., 1::2] << 4)).reshape(k // 512, 128, 2 * n)
    return np.ascontiguousarray(words), np.ascontiguousarray(byte.astype(np.uint8).reshape(k // 512, 16, n))


def unpack_weight(words, scales, fmt):
    g, _, n = scales.shape
    words = np.ascontiguousarray(words).reshape(g, 128, n, -1)
    if fmt == "e4m3":
        vals = words.view(ml_dtypes.float8_e4m3fn).astype(np.float64)
    else:
        nib = np.empty((g, 128, n, 4), np.uint8)
        nib[..., 0::2] = words & 0xF
        nib[..., 1::2] = words >> 4
        vals = E2M1[nib]
    vals = vals * np.repeat(np.exp2(scales.astype(np.float64) - 127.0), 8, axis=1)[..., None]
    return vals.transpose(0, 1, 3, 2).reshape(g * 512, n)


D, T, I, Q = 512, 1024, 512, 128


def setup_inputs():
    n = np.random.standard_normal
    idx = np.stack([np.random.permutation(T)[:I] for _ in range(8)])
    idx2 = np.stack([np.random.permutation(T)[:I] for _ in range(8)])
    idx3 = np.stack([np.random.permutation(T)[:I] for _ in range(8)])
    idx4 = np.stack([np.random.permutation(T)[:I] for _ in range(8)])
    fd = mx_kscale(D)
    keysp = pack_weight(n((D, T)) / fd[:, None], "e2m1")
    return {
        "query": (n((D, Q)) * 0.9 / np.sqrt(D) * fd[:, None]).astype(np.float32),
        "keys_words": keysp[0],
        "keys_scales": keysp[1],
        "lam": (np.random.uniform(0.7, 1.3, (Q, 1))).astype(np.float32),
        "old": (1.0 * n((Q, T))).astype(np.float32),
        "share2": (np.random.uniform(0.4, 1.2, (Q, 1))).astype(np.float32),
        "offs": striped8(idx),
        "offs2": striped8(idx2),
        "offs3": striped8(idx3),
        "offs4": striped8(idx4),
    }


def reference(query, keys_words, keys_scales, lam, old, share2, offs, offs2, offs3, offs4):
    idx = unstriped8(offs)
    idx2 = unstriped8(offs2)
    idx3 = unstriped8(offs3)
    idx4 = unstriped8(offs4)
    keysu = unpack_weight(keys_words, keys_scales, "e2m1")
    queryq = mxq(f64(query), 0, "e4m3")
    a = queryq.T @ keysu
    w = pick8(a, idx, 16) * f64(lam) - np.abs(pick8(a, idx2, 16) - pick8(a, idx3, 16))
    f1 = np.zeros((Q, T))
    f1[np.arange(Q)[:, None], idx[np.arange(Q) % 128 // 16]] = w
    f2 = np.zeros((Q, T))
    f2[np.arange(Q)[:, None], idx4[np.arange(Q) % 128 // 16]] = w
    y = f64(old) + f1 + f2 * f64(share2)
    return y

@@ -1,0 +1,170 @@
+from contextlib import ExitStack
+
+import concourse.mybir as mybir
+from concourse.masks import make_identity
+
+D, T, SLOTS, Q = 512, 1024, 512, 128
+FLOPS = 2 * D * T * Q
+
+F32 = mybir.dt.float32
+BF16 = mybir.dt.bfloat16
+I32 = mybir.dt.int32
+U32 = mybir.dt.uint32
+U16 = mybir.dt.uint16
+U8 = mybir.dt.uint8
+FP8X4 = mybir.dt.float8_e4m3fn_x4
+FP4X4 = mybir.dt.float4_e2m1fn_x4
+ALU = mybir.AluOpType
+COPY = mybir.ActivationFunctionType.Copy
+
+P = 128
+PACK = 4
+GROUP = 16
+HALF = SLOTS // 2
+N_MM = 256
+BANK = 512
+N_OUT = 256
+
+
+def tile_attend_betweentwo_lean_twiceput_heads_kernel(
+    tc, query, keys_words, keys_scales, lam, old, share2, offs, offs2, offs3, offs4, out
+):
+    nc = tc.nc
+    with ExitStack() as ctx:
+        lists = ctx.enter_context(tc.tile_pool(name="lists", bufs=1))
+        sb = ctx.enter_context(tc.tile_pool(name="sb", bufs=1))
+        ps = ctx.enter_context(tc.psum_pool(name="ps", bufs=1))
+
+        k_scales = sb.tile([P, T], U8, align_bytes=64)
+        nc.vector.memset(k_scales[:].bitcast(I32), 0)
+
+        q_raw = sb.tile([P, PACK, Q], F32, tag="staging")
+        nc.sync.dma_start(out=q_raw[:], in_=query.rearrange("(p j) q -> p j q", j=PACK))
+        k_words = sb.tile([P, 2 * T], U8, align_bytes=64)
+        nc.sync.dma_start(out=k_words[:].bitcast(I32), in_=keys_words[0].bitcast(I32))
+        for r in range(4):
+            nc.scalar.dma_start(
+                out=k_scales[r:P:32, :].bitcast(I32), in_=keys_scales[0, r:16:4, :].bitcast(I32)
+            )
+
+        list2 = lists.tile([P, SLOTS // GROUP], U16)
+        nc.sync.dma_start(list2[:], offs2)
+        list1 = lists.tile([P, SLOTS // GROUP], U16)
+        nc.sync.dma_start(list1[:], offs)
+        list3 = lists.tile([P, SLOTS // GROUP], U16)
+        nc.sync.dma_start(list3[:], offs3)
+        list4 = lists.tile([P, SLOTS // GROUP], U16)
+        nc.sync.dma_start(list4[:], offs4)
+        lam_col = sb.tile([P, 1], F32)
+        nc.gpsimd.dma_start(out=lam_col[:], in_=lam)
+        share_col = sb.tile([P, 1], F32)
+        nc.gpsimd.dma_start(out=share_col[:], in_=share2)
+
+        f1 = sb.tile([P, T], F32)
+        f2 = sb.tile([P, T], F32)
+        nc.vector.memset(f1[:], 0.0)
+        nc.vector.memset(f2[:], 0.0)
+        ident = sb.tile([P, P], F32)
+        make_identity(nc, ident[:])
+
+        q_bf = sb.tile([P, Q, PACK], BF16, align_bytes=64)
+        nc.vector.tensor_copy(
+            out=q_bf[:].rearrange("p (c i) j -> p c j i", i=4),
+            in_=q_raw[:].rearrange("p j (c i) -> p c j i", i=4),
+        )
+        q_codes = sb.tile([P, Q], U32, align_bytes=64)
+        q_scales = sb.tile([P, Q], U8, align_bytes=64)
+        nc.vector.quantize_mx(
+            out=q_codes[:].bitcast(FP8X4), scales=q_scales[:], in_=q_bf[:].rearrange("p q j -> p (q j)")
+        )
+
+        old_sb = sb.tile([P, T], F32, tag="staging")
+        nc.sync.dma_start(out=old_sb[:], in_=old)
+
+        lam_wide = sb.tile([P, HALF], F32)
+        nc.scalar.activation(lam_wide[:], lam_col[:].to_broadcast([P, HALF]), COPY)
+
+        a = sb.tile([P, T], F32)
+        for n in range(T // N_MM):
+            cols = slice(n * N_MM, (n + 1) * N_MM)
+            acc = ps.tile([P, N_MM], F32, name=f"acc{n}")
+            nc.tensor.matmul_mx(
+                out=acc[:],
+                lhsT=q_codes[:].bitcast(FP8X4),
+                lhsT_scale=q_scales[:],
+                rhs=k_words[:, 2 * n * N_MM : 2 * (n + 1) * N_MM].bitcast(FP4X4),
+                rhs_scale=k_scales[:, cols],
+                start=True,
+                stop=True,
+            )
+            if n % 2 == 0:
+                nc.scalar.copy(a[:, cols], acc[:])
+            else:
+                nc.vector.tensor_copy(a[:, cols], acc[:])
+
+        slots = [slice(0, HALF), slice(HALF, SLOTS)]
+        entries = [slice(0, HALF // GROUP), slice(HALF // GROUP, SLOTS // GROUP)]
+        second = sb.tile([P, SLOTS], F32)
+        first_raw = sb.tile([P, HALF], F32)
+        lead = sb.tile([P, SLOTS], F32)
+        diff = sb.tile([P, SLOTS], F32)
+        neg_abs = sb.tile([P, SLOTS], F32)
+
+        for h in range(2):
+            nc.scalar.activation(second[:, slots[h]], a[:].indirect(list2[:, entries[h]]), COPY)
+        nc.vector.tensor_tensor(lead[:, slots[0]], a[:].indirect(list1[:, entries[0]]), lam_wide[:], ALU.mult)
+        nc.scalar.activation(first_raw[:], a[:].indirect(list1[:, entries[1]]), COPY)
+        nc.scalar.activation(lead[:, slots[1]], first_raw[:], COPY, scale=lam_col[:])
+        for h in range(2):
+            nc.vector.tensor_tensor(
+                diff[:, slots[h]], a[:].indirect(list3[:, entries[h]]), second[:, slots[h]], ALU.subtract
+            )
+        for h in range(2):
+            nc.vector.scalar_tensor_tensor(
+                neg_abs[:, slots[h]], diff[:, slots[h]], -1.0, diff[:, slots[h]], ALU.mult, ALU.min
+            )
+
+        nc.vector.tensor_tensor(f1[:].indirect(list1[:]), lead[:], neg_abs[:], ALU.add)
+        nc.vector.tensor_tensor(f2[:].indirect(list4[:]), lead[:], neg_abs[:], ALU.add)
+
+        blocks = BANK // P
+        turned = [ps.tile([P, BANK], F32, name=f"turned{b}") for b in range(T // BANK)]
+        for b in range(T // BANK):
+            for j in range(blocks):
+                nc.tensor.matmul(
+                    turned[b][:, j * P : (j + 1) * P],
+                    old_sb[:, b * BANK + j * P : b * BANK + (j + 1) * P],
+                    ident[:],
+                    is_transpose=True,
+                    start=(j == 0),
+                    stop=False,
+                )
+        base_t = sb.tile([P, T], F32)
+        for b in range(T // BANK):
+            for j in range(blocks):
+                nc.tensor.matmul(
+                    turned[b][:, j * P : (j + 1) * P],
+                    f1[:, b * BANK + j * P : b * BANK + (j + 1) * P],
+                    ident[:],
+                    is_transpose=True,
+                    start=False,
+                    stop=(j == blocks - 1),
+                )
+            nc.scalar.copy(base_t[:, b * BANK : (b + 1) * BANK], turned[b][:])
+        base = [ps.tile([P, BANK], F32, name=f"base{b}") for b in range(T // BANK)]
+        for b in range(T // BANK):
+            for j in range(blocks):
+                nc.tensor.transpose(
+                    base[b][:, j * P : (j + 1) * P],
+                    base_t[:, b * BANK + j * P : b * BANK + (j + 1) * P],
+                    ident[:],
+                )
+
+        result = sb.tile([P, T], F32)
+        for n in range(T // N_OUT):
+            cols = slice(n * N_OUT, (n + 1) * N_OUT)
+            b, c0 = divmod(n * N_OUT, BANK)
+            nc.vector.scalar_tensor_tensor(
+                result[:, cols], f2[:, cols], share_col[:], base[b][:, c0 : c0 + N_OUT], ALU.mult, ALU.add
+            )
+            nc.sync.dma_start(out=out[:, cols], in_=result[:, cols])

@@ -16,6 +16,7 @@ FP8X4 = mybir.dt.float8_e4m3fn_x4
 FP4X4 = mybir.dt.float4_e2m1fn_x4
 ALU = mybir.AluOpType
 COPY = mybir.ActivationFunctionType.Copy
+ABS = mybir.ActivationFunctionType.Abs
 
 P = 128
 PACK = 4
@@ -36,17 +37,19 @@ def tile_attend_betweentwo_lean_twiceput_heads_kernel(
         ps = ctx.enter_context(tc.psum_pool(name="ps", bufs=1))
 
         k_scales = sb.tile([P, T], U8, align_bytes=64)
-        nc.vector.memset(k_scales[:].bitcast(I32), 0)
+        nc.gpsimd.memset(k_scales[:].bitcast(I32), 0)
 
-        q_raw = sb.tile([P, PACK, Q], F32, tag="staging")
+        q_raw = sb.tile([P, PACK, Q], F32)
         nc.sync.dma_start(out=q_raw[:], in_=query.rearrange("(p j) q -> p j q", j=PACK))
         k_words = sb.tile([P, 2 * T], U8, align_bytes=64)
         nc.sync.dma_start(out=k_words[:].bitcast(I32), in_=keys_words[0].bitcast(I32))
         for r in range(4):
-            nc.scalar.dma_start(
+            nc.sync.dma_start(
                 out=k_scales[r:P:32, :].bitcast(I32), in_=keys_scales[0, r:16:4, :].bitcast(I32)
             )
 
+        lam_col = sb.tile([P, 1], F32)
+        nc.sync.dma_start(out=lam_col[:], in_=lam)
         list2 = lists.tile([P, SLOTS // GROUP], U16)
         nc.sync.dma_start(list2[:], offs2)
         list1 = lists.tile([P, SLOTS // GROUP], U16)
@@ -55,19 +58,16 @@ def tile_attend_betweentwo_lean_twiceput_heads_kernel(
         nc.sync.dma_start(list3[:], offs3)
         list4 = lists.tile([P, SLOTS // GROUP], U16)
         nc.sync.dma_start(list4[:], offs4)
-        lam_col = sb.tile([P, 1], F32)
-        nc.gpsimd.dma_start(out=lam_col[:], in_=lam)
         share_col = sb.tile([P, 1], F32)
-        nc.gpsimd.dma_start(out=share_col[:], in_=share2)
+        nc.sync.dma_start(out=share_col[:], in_=share2)
 
-        f1 = sb.tile([P, T], F32)
-        f2 = sb.tile([P, T], F32)
-        nc.vector.memset(f1[:], 0.0)
-        nc.vector.memset(f2[:], 0.0)
+        f1 = [sb.tile([P, T], F32, name=f"f1_{h}") for h in range(2)]
+        for window in f1:
+            nc.vector.memset(window[:].bitcast(I32), 0)
         ident = sb.tile([P, P], F32)
         make_identity(nc, ident[:])
 
-        q_bf = sb.tile([P, Q, PACK], BF16, align_bytes=64)
+        q_bf = sb.tile([P, Q, PACK], BF16, align_bytes=64, tag="reused")
         nc.vector.tensor_copy(
             out=q_bf[:].rearrange("p (c i) j -> p c j i", i=4),
             in_=q_raw[:].rearrange("p j (c i) -> p c j i", i=4),
@@ -78,7 +78,9 @@ def tile_attend_betweentwo_lean_twiceput_heads_kernel(
             out=q_codes[:].bitcast(FP8X4), scales=q_scales[:], in_=q_bf[:].rearrange("p q j -> p (q j)")
         )
 
-        old_sb = sb.tile([P, T], F32, tag="staging")
+        f2 = sb.tile([P, T], F32, align_bytes=64, tag="reused")
+        nc.vector.memset(f2[:].bitcast(I32), 0)
+        old_sb = sb.tile([P, T], F32)
         nc.sync.dma_start(out=old_sb[:], in_=old)
 
         lam_wide = sb.tile([P, HALF], F32)
@@ -87,7 +89,7 @@ def tile_attend_betweentwo_lean_twiceput_heads_kernel(
         a = sb.tile([P, T], F32)
         for n in range(T // N_MM):
             cols = slice(n * N_MM, (n + 1) * N_MM)
-            acc = ps.tile([P, N_MM], F32, name=f"acc{n}")
+            acc = ps.tile([P, N_MM], F32, name=f"acc{n}", tag=f"quarter{n}")
             nc.tensor.matmul_mx(
                 out=acc[:],
                 lhsT=q_codes[:].bitcast(FP8X4),
@@ -102,69 +104,62 @@ def tile_attend_betweentwo_lean_twiceput_heads_kernel(
             else:
                 nc.vector.tensor_copy(a[:, cols], acc[:])
 
-        slots = [slice(0, HALF), slice(HALF, SLOTS)]
-        entries = [slice(0, HALF // GROUP), slice(HALF // GROUP, SLOTS // GROUP)]
+        lo, hi = slice(0, HALF), slice(HALF, SLOTS)
+        lo_entries, hi_entries = slice(0, HALF // GROUP), slice(HALF // GROUP, SLOTS // GROUP)
         second = sb.tile([P, SLOTS], F32)
-        first_raw = sb.tile([P, HALF], F32)
         lead = sb.tile([P, SLOTS], F32)
         diff = sb.tile([P, SLOTS], F32)
         neg_abs = sb.tile([P, SLOTS], F32)
+        first_hi = sb.tile([P, HALF], F32)
+        third_hi = sb.tile([P, HALF], F32)
+        abs_hi = sb.tile([P, HALF], F32)
 
-        for h in range(2):
-            nc.scalar.activation(second[:, slots[h]], a[:].indirect(list2[:, entries[h]]), COPY)
-        nc.vector.tensor_tensor(lead[:, slots[0]], a[:].indirect(list1[:, entries[0]]), lam_wide[:], ALU.mult)
-        nc.scalar.activation(first_raw[:], a[:].indirect(list1[:, entries[1]]), COPY)
-        nc.scalar.activation(lead[:, slots[1]], first_raw[:], COPY, scale=lam_col[:])
-        for h in range(2):
-            nc.vector.tensor_tensor(
-                diff[:, slots[h]], a[:].indirect(list3[:, entries[h]]), second[:, slots[h]], ALU.subtract
-            )
-        for h in range(2):
-            nc.vector.scalar_tensor_tensor(
-                neg_abs[:, slots[h]], diff[:, slots[h]], -1.0, diff[:, slots[h]], ALU.mult, ALU.min
-            )
+        nc.scalar.activation(second[:, lo], a[:].indirect(list2[:, lo_entries]), COPY)
+        nc.vector.tensor_tensor(lead[:, lo], a[:].indirect(list1[:, lo_entries]), lam_wide[:], ALU.mult)
+        nc.vector.tensor_tensor(diff[:, lo], a[:].indirect(list3[:, lo_entries]), second[:, lo], ALU.subtract)
+        nc.vector.scalar_tensor_tensor(neg_abs[:, lo], diff[:, lo], -1.0, diff[:, lo], ALU.mult, ALU.min)
 
-        nc.vector.tensor_tensor(f1[:].indirect(list1[:]), lead[:], neg_abs[:], ALU.add)
+        nc.scalar.activation(second[:, hi], a[:].indirect(list2[:, hi_entries]), COPY)
+        nc.scalar.activation(third_hi[:], a[:].indirect(list3[:, hi_entries]), COPY)
+        nc.vector.tensor_tensor(diff[:, hi], second[:, hi], third_hi[:], ALU.subtract)
+        nc.scalar.activation(first_hi[:], a[:].indirect(list1[:, hi_entries]), COPY)
+        nc.scalar.activation(abs_hi[:], diff[:, hi], ABS)
+        nc.scalar.activation(lead[:, hi], first_hi[:], COPY, scale=lam_col[:])
+        nc.scalar.activation(neg_abs[:, hi], abs_hi[:], COPY, scale=-1.0)
+
+        nc.vector.tensor_tensor(f1[0][:].indirect(list1[:, lo_entries]), lead[:, lo], neg_abs[:, lo], ALU.add)
+        nc.vector.tensor_tensor(f1[1][:].indirect(list1[:, hi_entries]), lead[:, hi], neg_abs[:, hi], ALU.add)
         nc.vector.tensor_tensor(f2[:].indirect(list4[:]), lead[:], neg_abs[:], ALU.add)
 
-        blocks = BANK // P
-        turned = [ps.tile([P, BANK], F32, name=f"turned{b}") for b in range(T // BANK)]
-        for b in range(T // BANK):
-            for j in range(blocks):
-                nc.tensor.matmul(
-                    turned[b][:, j * P : (j + 1) * P],
-                    old_sb[:, b * BANK + j * P : b * BANK + (j + 1) * P],
-                    ident[:],
-                    is_transpose=True,
-                    start=(j == 0),
-                    stop=False,
-                )
+        quarters = T // N_MM
+        blocks = N_MM // P
+        turned = [ps.tile([P, N_MM], F32, name=f"turned{n}") for n in range(quarters)]
         base_t = sb.tile([P, T], F32)
-        for b in range(T // BANK):
-            for j in range(blocks):
-                nc.tensor.matmul(
-                    turned[b][:, j * P : (j + 1) * P],
-                    f1[:, b * BANK + j * P : b * BANK + (j + 1) * P],
-                    ident[:],
-                    is_transpose=True,
-                    start=False,
-                    stop=(j == blocks - 1),
-                )
-            nc.scalar.copy(base_t[:, b * BANK : (b + 1) * BANK], turned[b][:])
-        base = [ps.tile([P, BANK], F32, name=f"base{b}") for b in range(T // BANK)]
-        for b in range(T // BANK):
-            for j in range(blocks):
-                nc.tensor.transpose(
-                    base[b][:, j * P : (j + 1) * P],
-                    base_t[:, b * BANK + j * P : b * BANK + (j + 1) * P],
-                    ident[:],
-                )
-
+        terms = (old_sb, f1[0], f1[1])
+        for k, term in enumerate(terms):
+            for n in range(quarters):
+                for j in range(blocks):
+                    c0 = n * N_MM + j * P
+                    nc.tensor.matmul(
+                        turned[n][:, j * P : (j + 1) * P],
+                        term[:, c0 : c0 + P],
+                        ident[:],
+                        is_transpose=True,
+                        start=(k == 0 and j == 0),
+                        stop=(k == len(terms) - 1 and j == blocks - 1),
+                    )
         result = sb.tile([P, T], F32)
-        for n in range(T // N_OUT):
-            cols = slice(n * N_OUT, (n + 1) * N_OUT)
-            b, c0 = divmod(n * N_OUT, BANK)
-            nc.vector.scalar_tensor_tensor(
-                result[:, cols], f2[:, cols], share_col[:], base[b][:, c0 : c0 + N_OUT], ALU.mult, ALU.add
-            )
+        base = []
+        for n in range(quarters):
+            cols = slice(n * N_MM, (n + 1) * N_MM)
+            nc.scalar.copy(base_t[:, cols], turned[n][:])
+        for n in range(quarters):
+            bank = ps.tile([P, N_MM], F32, name=f"base{n}", tag=f"quarter{n}")
+            for j in range(blocks):
+                c0 = n * N_MM + j * P
+                nc.tensor.transpose(bank[:, j * P : (j + 1) * P], base_t[:, c0 : c0 + P], ident[:])
+            base.append(bank)
+        for n in range(quarters):
+            cols = slice(n * N_MM, (n + 1) * N_MM)
+            nc.vector.scalar_tensor_tensor(result[:, cols], f2[:, cols], share_col[:], base[n][:], ALU.mult, ALU.add)
             nc.sync.dma_start(out=out[:, cols], in_=result[:, cols])

@@ -37,19 +37,17 @@ def tile_attend_betweentwo_lean_twiceput_heads_kernel(
         ps = ctx.enter_context(tc.psum_pool(name="ps", bufs=1))
 
         k_scales = sb.tile([P, T], U8, align_bytes=64)
-        nc.gpsimd.memset(k_scales[:].bitcast(I32), 0)
+        nc.vector.memset(k_scales[:].bitcast(I32), 0)
 
-        q_raw = sb.tile([P, PACK, Q], F32)
+        q_raw = sb.tile([P, PACK, Q], F32, tag="staging")
         nc.sync.dma_start(out=q_raw[:], in_=query.rearrange("(p j) q -> p j q", j=PACK))
         k_words = sb.tile([P, 2 * T], U8, align_bytes=64)
         nc.sync.dma_start(out=k_words[:].bitcast(I32), in_=keys_words[0].bitcast(I32))
         for r in range(4):
-            nc.sync.dma_start(
+            nc.scalar.dma_start(
                 out=k_scales[r:P:32, :].bitcast(I32), in_=keys_scales[0, r:16:4, :].bitcast(I32)
             )
 
-        lam_col = sb.tile([P, 1], F32)
-        nc.sync.dma_start(out=lam_col[:], in_=lam)
         list2 = lists.tile([P, SLOTS // GROUP], U16)
         nc.sync.dma_start(list2[:], offs2)
         list1 = lists.tile([P, SLOTS // GROUP], U16)
@@ -58,8 +56,10 @@ def tile_attend_betweentwo_lean_twiceput_heads_kernel(
         nc.sync.dma_start(list3[:], offs3)
         list4 = lists.tile([P, SLOTS // GROUP], U16)
         nc.sync.dma_start(list4[:], offs4)
+        lam_col = sb.tile([P, 1], F32)
+        nc.gpsimd.dma_start(out=lam_col[:], in_=lam)
         share_col = sb.tile([P, 1], F32)
-        nc.sync.dma_start(out=share_col[:], in_=share2)
+        nc.gpsimd.dma_start(out=share_col[:], in_=share2)
 
         f1 = [sb.tile([P, T], F32, name=f"f1_{h}") for h in range(2)]
         for window in f1:
@@ -80,7 +80,7 @@ def tile_attend_betweentwo_lean_twiceput_heads_kernel(
 
         f2 = sb.tile([P, T], F32, align_bytes=64, tag="reused")
         nc.vector.memset(f2[:].bitcast(I32), 0)
-        old_sb = sb.tile([P, T], F32)
+        old_sb = sb.tile([P, T], F32, tag="staging")
         nc.sync.dma_start(out=old_sb[:], in_=old)
 
         lam_wide = sb.tile([P, HALF], F32)

from contextlib import ExitStack

import concourse.mybir as mybir
from concourse.masks import make_identity

D, T, SLOTS, Q = 512, 1024, 512, 128
FLOPS = 2 * D * T * Q

F32 = mybir.dt.float32
BF16 = mybir.dt.bfloat16
I32 = mybir.dt.int32
U32 = mybir.dt.uint32
U16 = mybir.dt.uint16
U8 = mybir.dt.uint8
FP8X4 = mybir.dt.float8_e4m3fn_x4
FP4X4 = mybir.dt.float4_e2m1fn_x4
ALU = mybir.AluOpType
COPY = mybir.ActivationFunctionType.Copy
ABS = mybir.ActivationFunctionType.Abs

P = 128
PACK = 4
GROUP = 16
HALF = SLOTS // 2
N_MM = 256
BANK = 512
N_OUT = 256


def tile_attend_betweentwo_lean_twiceput_heads_kernel(
    tc, query, keys_words, keys_scales, lam, old, share2, offs, offs2, offs3, offs4, out
):
    nc = tc.nc
    with ExitStack() as ctx:
        lists = ctx.enter_context(tc.tile_pool(name="lists", bufs=1))
        sb = ctx.enter_context(tc.tile_pool(name="sb", bufs=1))
        ps = ctx.enter_context(tc.psum_pool(name="ps", bufs=1))

        k_scales = sb.tile([P, T], U8, align_bytes=64)
        nc.vector.memset(k_scales[:].bitcast(I32), 0)

        q_raw = sb.tile([P, PACK, Q], F32, tag="staging")
        nc.sync.dma_start(out=q_raw[:], in_=query.rearrange("(p j) q -> p j q", j=PACK))
        k_words = sb.tile([P, 2 * T], U8, align_bytes=64)
        nc.sync.dma_start(out=k_words[:].bitcast(I32), in_=keys_words[0].bitcast(I32))
        for r in range(4):
            nc.scalar.dma_start(
                out=k_scales[r:P:32, :].bitcast(I32), in_=keys_scales[0, r:16:4, :].bitcast(I32)
            )

        list2 = lists.tile([P, SLOTS // GROUP], U16)
        nc.sync.dma_start(list2[:], offs2)
        list1 = lists.tile([P, SLOTS // GROUP], U16)
        nc.sync.dma_start(list1[:], offs)
        list3 = lists.tile([P, SLOTS // GROUP], U16)
        nc.sync.dma_start(list3[:], offs3)
        list4 = lists.tile([P, SLOTS // GROUP], U16)
        nc.sync.dma_start(list4[:], offs4)
        lam_col = sb.tile([P, 1], F32)
        nc.gpsimd.dma_start(out=lam_col[:], in_=lam)
        share_col = sb.tile([P, 1], F32)
        nc.gpsimd.dma_start(out=share_col[:], in_=share2)

        f1 = [sb.tile([P, T], F32, name=f"f1_{h}") for h in range(2)]
        for window in f1:
            nc.vector.memset(window[:].bitcast(I32), 0)
        ident = sb.tile([P, P], F32)
        make_identity(nc, ident[:])

        q_bf = sb.tile([P, Q, PACK], BF16, align_bytes=64, tag="reused")
        nc.vector.tensor_copy(
            out=q_bf[:].rearrange("p (c i) j -> p c j i", i=4),
            in_=q_raw[:].rearrange("p j (c i) -> p c j i", i=4),
        )
        q_codes = sb.tile([P, Q], U32, align_bytes=64)
        q_scales = sb.tile([P, Q], U8, align_bytes=64)
        nc.vector.quantize_mx(
            out=q_codes[:].bitcast(FP8X4), scales=q_scales[:], in_=q_bf[:].rearrange("p q j -> p (q j)")
        )

        f2 = sb.tile([P, T], F32, align_bytes=64, tag="reused")
        nc.vector.memset(f2[:].bitcast(I32), 0)
        old_sb = sb.tile([P, T], F32, tag="staging")
        nc.sync.dma_start(out=old_sb[:], in_=old)

        lam_wide = sb.tile([P, HALF], F32)
        nc.scalar.activation(lam_wide[:], lam_col[:].to_broadcast([P, HALF]), COPY)

        a = sb.tile([P, T], F32)
        for n in range(T // N_MM):
            cols = slice(n * N_MM, (n + 1) * N_MM)
            acc = ps.tile([P, N_MM], F32, name=f"acc{n}", tag=f"quarter{n}")
            nc.tensor.matmul_mx(
                out=acc[:],
                lhsT=q_codes[:].bitcast(FP8X4),
                lhsT_scale=q_scales[:],
                rhs=k_words[:, 2 * n * N_MM : 2 * (n + 1) * N_MM].bitcast(FP4X4),
                rhs_scale=k_scales[:, cols],
                start=True,
                stop=True,
            )
            if n % 2 == 0:
                nc.scalar.copy(a[:, cols], acc[:])
            else:
                nc.vector.tensor_copy(a[:, cols], acc[:])

        lo, hi = slice(0, HALF), slice(HALF, SLOTS)
        lo_entries, hi_entries = slice(0, HALF // GROUP), slice(HALF // GROUP, SLOTS // GROUP)
        second = sb.tile([P, SLOTS], F32)
        lead = sb.tile([P, SLOTS], F32)
        diff = sb.tile([P, SLOTS], F32)
        neg_abs = sb.tile([P, SLOTS], F32)
        first_hi = sb.tile([P, HALF], F32)
        third_hi = sb.tile([P, HALF], F32)
        abs_hi = sb.tile([P, HALF], F32)

        nc.scalar.activation(second[:, lo], a[:].indirect(list2[:, lo_entries]), COPY)
        nc.vector.tensor_tensor(lead[:, lo], a[:].indirect(list1[:, lo_entries]), lam_wide[:], ALU.mult)
        nc.vector.tensor_tensor(diff[:, lo], a[:].indirect(list3[:, lo_entries]), second[:, lo], ALU.subtract)
        nc.vector.scalar_tensor_tensor(neg_abs[:, lo], diff[:, lo], -1.0, diff[:, lo], ALU.mult, ALU.min)

        nc.scalar.activation(second[:, hi], a[:].indirect(list2[:, hi_entries]), COPY)
        nc.scalar.activation(third_hi[:], a[:].indirect(list3[:, hi_entries]), COPY)
        nc.vector.tensor_tensor(diff[:, hi], second[:, hi], third_hi[:], ALU.subtract)
        nc.scalar.activation(first_hi[:], a[:].indirect(list1[:, hi_entries]), COPY)
        nc.scalar.activation(abs_hi[:], diff[:, hi], ABS)
        nc.scalar.activation(lead[:, hi], first_hi[:], COPY, scale=lam_col[:])
        nc.scalar.activation(neg_abs[:, hi], abs_hi[:], COPY, scale=-1.0)

        nc.vector.tensor_tensor(f1[0][:].indirect(list1[:, lo_entries]), lead[:, lo], neg_abs[:, lo], ALU.add)
        nc.vector.tensor_tensor(f1[1][:].indirect(list1[:, hi_entries]), lead[:, hi], neg_abs[:, hi], ALU.add)
        nc.vector.tensor_tensor(f2[:].indirect(list4[:]), lead[:], neg_abs[:], ALU.add)

        quarters = T // N_MM
        blocks = N_MM // P
        turned = [ps.tile([P, N_MM], F32, name=f"turned{n}") for n in range(quarters)]
        base_t = sb.tile([P, T], F32)
        terms = (old_sb, f1[0], f1[1])
        for k, term in enumerate(terms):
            for n in range(quarters):
                for j in range(blocks):
                    c0 = n * N_MM + j * P
                    nc.tensor.matmul(
                        turned[n][:, j * P : (j + 1) * P],
                        term[:, c0 : c0 + P],
                        ident[:],
                        is_transpose=True,
                        start=(k == 0 and j == 0),
                        stop=(k == len(terms) - 1 and j == blocks - 1),
                    )
        result = sb.tile([P, T], F32)
        base = []
        for n in range(quarters):
            cols = slice(n * N_MM, (n + 1) * N_MM)
            nc.scalar.copy(base_t[:, cols], turned[n][:])
        for n in range(quarters):
            bank = ps.tile([P, N_MM], F32, name=f"base{n}", tag=f"quarter{n}")
            for j in range(blocks):
                c0 = n * N_MM + j * P
                nc.tensor.transpose(bank[:, j * P : (j + 1) * P], base_t[:, c0 : c0 + P], ident[:])
            base.append(bank)
        for n in range(quarters):
            cols = slice(n * N_MM, (n + 1) * N_MM)
            nc.vector.scalar_tensor_tensor(result[:, cols], f2[:, cols], share_col[:], base[n][:], ALU.mult, ALU.add)
            nc.sync.dma_start(out=out[:, cols], in_=result[:, cols])
